import numpy as np
import ml_dtypes


def mxq(x, axis, fmt="e4m3"):
    dtype, down = {"e4m3": (ml_dtypes.float8_e4m3fn, 7), "e5m2": (ml_dtypes.float8_e5m2, 14)}[fmt]
    v = np.moveaxis(np.asarray(x, np.float32).astype(ml_dtypes.bfloat16).astype(np.float64), axis, -1)
    blocks = v.reshape(v.shape[:-1] + (-1, 32))
    amax = np.abs(blocks).max(-1, keepdims=True)
    byte = np.maximum(np.where(amax > 0, np.frexp(amax)[1] - 1 + 127, 0) - down, 1)
    scale = np.exp2(byte - 127.0)
    codes = (blocks / scale).astype(np.float32).astype(dtype).astype(np.float64)
    return np.moveaxis((codes * scale).reshape(v.shape), -1, axis)


WIDE = False


def mx_kscale(k):
    if not WIDE:
        return np.ones(k)
    levels = np.array([10, -10, 5, -5, 0])
    if k % 512:
        return np.exp2(np.random.permutation(np.resize(levels, k // 32))).repeat(32)
    a = np.empty((k // 512, 16))
    for p in range(k // 512):
        a[p, :8] = np.random.permutation(np.resize(levels, 8))
        for g in range(8):
            far = levels[np.abs(levels - a[p, g]) >= 10]
            a[p, g + 8] = far[np.random.randint(len(far))]
    return np.exp2(a.ravel()).repeat(32)


def f64(x):
    return np.asarray(x).astype(np.float64)


def striped(idx):
    return np.tile(idx.reshape(-1, 16).T, (8, 1)).astype(np.uint16)


def unstriped(offs):
    return offs[:16].T.reshape(-1).astype(np.int64)


def pack_weight(w):
    k, n = w.shape
    w = f64(np.asarray(w, np.float32).astype(ml_dtypes.bfloat16)).reshape(k // 32, 32, n)
    amax = np.abs(w).max(1)
    byte = np.clip(np.where(amax > 0, np.frexp(amax)[1] - 1 + 127 - 7, 1), 1, 254)
    scaled = (w * np.exp2(127.0 - byte)[:, None, :]).reshape(k, n).astype(np.float32)
    words = np.ascontiguousarray(scaled.reshape(k // 512, 128, 4, n).transpose(0, 1, 3, 2)).astype(ml_dtypes.float8_e4m3fn).view(np.uint8)
    return words, np.ascontiguousarray(byte.astype(np.uint8).reshape(k // 512, 16, n))


def unpack_weight(words, scales):
    g, p, n, _ = words.shape
    vals = np.ascontiguousarray(words).view(ml_dtypes.float8_e4m3fn).astype(np.float64) * np.repeat(np.exp2(scales.astype(np.float64) - 127.0), 8, axis=1)[..., None]
    return vals.transpose(0, 1, 3, 2).reshape(g * 512, n)


K, T, E, C, N = 1536, 512, 8, 128, 512


def by_expert(wq, xq):
    return np.concatenate([wq[e].T @ xq[:, e * C:(e + 1) * C] for e in range(E)], axis=1)


def setup_inputs():
    n = np.random.standard_normal
    s = mx_kscale(K)[:, None]
    first = np.random.permutation(np.repeat(np.arange(E), T // E))
    second = (first + 1 + np.random.permutation(np.repeat(np.arange(E - 1), -(-T // (E - 1)))[:T])) % E
    while np.bincount(second, minlength=E).max() != T // E:
        load = np.bincount(second, minlength=E); hi, lo = int(load.argmax()), int(load.argmin())
        t = np.flatnonzero((second == hi) & (first != lo))[0]; second[t] = lo
    slot_token = np.empty(E * C, np.int64); pos = np.empty((2, T), np.int64); fill = np.zeros(E, np.int64)
    place = np.stack([np.random.permutation(C) for _ in range(E)])
    for r, deal in enumerate((first, second)):
        for t in np.random.permutation(T):
            e = deal[t]; j = e * C + place[e, fill[e]]; fill[e] += 1; slot_token[j] = t; pos[r, t] = j
    g = np.random.uniform(0.2, 0.8, T)
    packed = [pack_weight(m) for m in n((E, K, N)) / np.sqrt(K) / s[None]]
    return {
        "xT": (n((K, T)) * s).astype(np.float32),
        "w_words": np.stack([m[0] for m in packed]),
        "w_scales": np.stack([m[1] for m in packed]),
        "b": (0.3 * n((N, E))).astype(np.float32),
        "gate": np.stack([np.tile(g, (N, 1)), np.tile(1.0 - g, (N, 1))]).astype(np.float32),
        "offs": striped(slot_token),
        "pos1": striped(pos[0]),
        "pos2": striped(pos[1]),
    }


def reference(xT, w_words, w_scales, b, gate, offs, pos1, pos2):
    idx = unstriped(offs)
    xq = mxq(f64(xT)[:, idx], 0, "e4m3")
    w = np.stack([unpack_weight(w_words[e], w_scales[e]) for e in range(E)])
    y = by_expert(w, xq)
    y = y + np.repeat(f64(b), C, axis=1)
    return f64(gate[0]) * y[:, unstriped(pos1)] + f64(gate[1]) * y[:, unstriped(pos2)]

from contextlib import ExitStack

import concourse.mybir as mybir

K, T, E, C, N = 1536, 512, 8, 128, 512
S = E * C
P = 128
PASS = 512
NPASS = K // PASS
NB = N // P
FLOPS = 2 * K * N * S + 3 * N * T + N * S
BYTES = 4 * K * T + E * K * N + E * K * N // 32 + 4 * N * E + 4 * 2 * T + 2 * P * (S + 2 * T) // 16 + 4 * N * T

F32 = mybir.dt.float32
BF16 = mybir.dt.bfloat16
I32 = mybir.dt.int32
U32 = mybir.dt.uint32
U16 = mybir.dt.uint16
U8 = mybir.dt.uint8
X4 = mybir.dt.float8_e4m3fn_x4
MULT = mybir.AluOpType.mult
ADD = mybir.AluOpType.add
IDENT = mybir.ActivationFunctionType.Identity


def tile_routed_moe_kernel(tc, xT, w_words, w_scales, b, gate, offs, pos1, pos2, out):
    nc = tc.nc
    with ExitStack() as ctx:
        keep = ctx.enter_context(tc.tile_pool(name="keep", bufs=1))
        psum = ctx.enter_context(tc.psum_pool(name="psum", bufs=8))

        offs_t = keep.tile([P, S // 16], U16, name="offs_t")
        pos1_t = keep.tile([P, T // 16], U16, name="pos1_t")
        pos2_t = keep.tile([P, T // 16], U16, name="pos2_t")
        raw = [keep.tile([P, 4, T], F32, name=f"raw{a}") for a in range(NPASS)]
        grouped = [keep.tile([P, T, 4], BF16, name=f"grouped{a}", align_bytes=64) for a in range(NPASS)]
        words = [keep.tile([P, T], U32, name=f"words{a}", align_bytes=64) for a in range(NPASS)]
        planes = keep.tile([P, T], U8, name="planes", align_bytes=64)
        slot_words = keep.tile([P, NPASS, S], U32, name="slot_words", align_bytes=64)
        slot_planes = keep.tile([P, S], U8, name="slot_planes", align_bytes=64)
        w_planes = keep.tile([P, E, N], U8, name="w_planes", align_bytes=64)
        bias = keep.tile([P, NB, E], F32, name="bias")
        gates = keep.tile([P, 2, T], F32, name="gates")
        sums = [keep.tile([P, S], F32, name=f"sums{q}") for q in range(NB)]

        nc.vector.memset(planes[:].bitcast(I32), 0)
        nc.vector.memset(w_planes[:].rearrange("p e n -> p (e n)").bitcast(I32), 0)
        nc.gpsimd.dma_start(bias[:], b.rearrange("(q p) e -> p q e", p=P))

        nc.sync.dma_start(offs_t[:], offs)
        half = T // 2
        for a in range(NPASS):
            rows = xT[a * PASS : (a + 1) * PASS, :].rearrange("(p j) t -> p j t", j=4)
            if a == 0:
                for t0 in (0, half):
                    nc.sync.dma_start(raw[a][:, :, t0 : t0 + half], rows[:, :, t0 : t0 + half])
            else:
                nc.sync.dma_start(raw[a][:], rows)
        for a in range(NPASS):
            for r in range(4):
                nc.sync.dma_start(
                    w_planes[4 * a + r : P : 32, :, :].bitcast(I32),
                    w_scales[:, a, r:16:4, :].rearrange("e q n -> q e n").bitcast(I32),
                )

        def load_w(e, n0, width):
            t = keep.tile([P, NPASS, width], U32, name=f"w{e}_{n0}", align_bytes=64)
            nc.sync.dma_start(
                t[:].bitcast(I32),
                w_words[e][:, :, n0 : n0 + width, :].rearrange("a p n r -> p a (n r)").bitcast(I32),
            )
            return [(t, i) for i in range(width // P)]

        weights = {}
        for e in range(E):
            weights[e, 0], weights[e, 1] = load_w(e, 0, 2 * P)
        nc.sync.dma_start(gates[:], gate[:, 0:P, :].rearrange("g p t -> p g t"))
        nc.sync.dma_start(pos1_t[:], pos1)
        nc.sync.dma_start(pos2_t[:], pos2)
        for e in range(4):
            weights[e, 2], weights[e, 3] = load_w(e, 2 * P, 2 * P)
        for q in (2, 3):
            for e in range(4, E):
                weights[e, q] = load_w(e, q * P, P)[0]

        def interleave(copy, a, t0, t1):
            copy(
                grouped[a][:, t0:t1, :].rearrange("p (c i) j -> p c j i", i=4),
                raw[a][:, :, t0:t1].rearrange("p j (c i) -> p c j i", i=4),
            )

        def quantize(a):
            nc.vector.quantize_mx(
                out=words[a][:].bitcast(X4),
                scales=planes[4 * a : P, :],
                in_=grouped[a][:].rearrange("p t j -> p (t j)"),
            )

        cuts = ((0, 384), (384, 768), (768, 1024))

        def gather_words(a, s0, s1):
            nc.vector.tensor_copy(slot_words[:, a, s0:s1], words[a][:].indirect(offs_t[:, s0 // 16 : s1 // 16]))

        def gather_planes(s0, s1):
            nc.vector.tensor_copy(slot_planes[:, s0:s1], planes[:].indirect(offs_t[:, s0 // 16 : s1 // 16]))

        interleave(nc.vector.tensor_copy, 0, 0, half)
        interleave(nc.scalar.copy, 0, half, T)
        for a in range(1, NPASS):
            interleave(nc.scalar.copy, a, 0, half)
            interleave(nc.scalar.copy, a, half, T)
        for a in range(NPASS - 1):
            quantize(a)
            for s0, s1 in cuts:
                gather_words(a, s0, s1)
        quantize(NPASS - 1)
        for s0, s1 in cuts:
            gather_words(NPASS - 1, s0, s1)
            gather_planes(s0, s1)

        def expert(q, e):
            acc = psum.tile([P, C], F32, name="acc")
            t, i = weights[e, q]
            slots = slice(e * C, (e + 1) * C)
            for a in range(NPASS):
                nc.tensor.matmul_mx(
                    out=acc[:],
                    lhsT=t[:, a, i * P : (i + 1) * P].bitcast(X4),
                    lhsT_scale=w_planes[4 * a : P, e, q * P : (q + 1) * P],
                    rhs=slot_words[:, a, slots].bitcast(X4),
                    rhs_scale=slot_planes[4 * a : P, slots],
                    start=(a == 0),
                    stop=(a == NPASS - 1),
                )
            nc.scalar.activation(sums[q][:, slots], acc[:], IDENT, bias=bias[:, q, e : e + 1])

        def combine(q):
            first = keep.tile([P, T], F32, name=f"first{q}")
            second = keep.tile([P, T], F32, name=f"second{q}")
            both = keep.tile([P, T], F32, name=f"both{q}")
            nc.vector.tensor_tensor(first[:], sums[q][:].indirect(pos1_t[:]), gates[:, 0, :], MULT)
            nc.vector.tensor_tensor(second[:], sums[q][:].indirect(pos2_t[:]), gates[:, 1, :], MULT)
            nc.vector.tensor_tensor(both[:], first[:], second[:], ADD)
            nc.sync.dma_start(out[q * P : (q + 1) * P, :], both[:])

        for e in range(E):
            expert(0, e)
            expert(1, e)
        combine(0)
        combine(1)
        for e in range(4):
            expert(2, e)
            expert(3, e)
        for q in (2, 3):
            for e in range(4, E):
                expert(q, e)
            combine(q)
